import numpy as np
import ml_dtypes


def mxq(x, axis, fmt="e4m3"):
    dtype, down = {"e4m3": (ml_dtypes.float8_e4m3fn, 7), "e5m2": (ml_dtypes.float8_e5m2, 14)}[fmt]
    v = np.moveaxis(np.asarray(x, np.float32).astype(ml_dtypes.bfloat16).astype(np.float64), axis, -1)
    blocks = v.reshape(v.shape[:-1] + (-1, 32))
    amax = np.abs(blocks).max(-1, keepdims=True)
    byte = np.maximum(np.where(amax > 0, np.frexp(amax)[1] - 1 + 127, 0) - down, 1)
    scale = np.exp2(byte - 127.0)
    codes = (blocks / scale).astype(np.float32).astype(dtype).astype(np.float64)
    return np.moveaxis((codes * scale).reshape(v.shape), -1, axis)


WIDE = False


def mx_kscale(k):
    if not WIDE:
        return np.ones(k)
    levels = np.array([30, -30])
    if k % 512:
        return np.exp2(np.random.permutation(np.resize(levels, k // 32))).repeat(32)
    a = np.empty((k // 512, 16))
    for p in range(k // 512):
        a[p, :8] = np.random.permutation(np.resize(levels, 8))
        for g in range(8):
            far = levels[np.abs(levels - a[p, g]) >= 10]
            a[p, g + 8] = far[np.random.randint(len(far))]
    return np.exp2(a.ravel()).repeat(32)


def f64(x):
    return np.asarray(x).astype(np.float64)


def striped(idx):
    return np.tile(np.asarray(idx).reshape(-1, 16).T, (8, 1)).astype(np.uint16)


def unstriped(offs):
    return offs[:16].T.reshape(-1).astype(np.int64)


def striped8(idx):
    return np.asarray(idx).reshape(8, -1, 16).transpose(0, 2, 1).reshape(128, -1).astype(np.uint16)


def unstriped8(offs):
    return offs.reshape(8, 16, -1).transpose(0, 2, 1).reshape(8, -1).astype(np.int64)


def pick8(x, idx, run):
    r = np.arange(len(x))
    return x[r[:, None], idx[r % (8 * run) // run]]


E2M1 = np.array([0.0, 0.5, 1.0, 1.5, 2.0, 3.0, 4.0, 6.0, -0.0, -0.5, -1.0, -1.5, -2.0, -3.0, -4.0, -6.0])


def pack_weight(w, fmt):
    k, n = w.shape
    w = f64(np.asarray(w, np.float32).astype(ml_dtypes.bfloat16)).reshape(k // 32, 32, n)
    amax = np.abs(w).max(1)
    if fmt in ("e4m3", "e5m2"):
        byte = np.frexp(amax)[1] - 1 + 127 - (7 if fmt == "e4m3" else 14)
    else:
        mant, ex = np.frexp(amax / 6.0)
        byte = np.where(mant > 0.5, ex, ex - 1) + 127
    byte = np.clip(np.where(amax > 0, byte, 1), 1, 254)
    scaled = (w * np.exp2(127.0 - byte)[:, None, :]).reshape(k, n).astype(np.float32)
    by_word = np.ascontiguousarray(scaled.reshape(k // 512, 128, 4, n).transpose(0, 1, 3, 2))
    if fmt in ("e4m3", "e5m2"):
        words = by_word.astype(ml_dtypes.float8_e4m3fn if fmt == "e4m3" else ml_dtypes.float8_e5m2).view(np.uint8)
    else:
        c = by_word.astype(ml_dtypes.float4_e2m1fn).view(np.uint8) & 0xF
        words = (c[..., 0::2] | (c[..., 1::2] << 4)).reshape(k // 512, 128, 2 * n)
    return np.ascontiguousarray(words), np.ascontiguousarray(byte.astype(np.uint8).reshape(k // 512, 16, n))


def unpack_weight(words, scales, fmt):
    g, _, n = scales.shape
    words = np.ascontiguousarray(words).reshape(g, 128, n, -1)
    if fmt in ("e4m3", "e5m2"):
        vals = words.view(ml_dtypes.float8_e4m3fn if fmt == "e4m3" else ml_dtypes.float8_e5m2).astype(np.float64)
    else:
        nib = np.empty((g, 128, n, 4), np.uint8)
        nib[..., 0::2] = words & 0xF
        nib[..., 1::2] = words >> 4
        vals = E2M1[nib]
    vals = vals * np.repeat(np.exp2(scales.astype(np.float64) - 127.0), 8, axis=1)[..., None]
    return vals.transpose(0, 1, 3, 2).reshape(g * 512, n)


K, T, J, R, F, Z, C, O, N, S, E = 512, 1024, 256, 512, 512, 1024, 512, 128, 256, 1024, 1024


def setup_inputs():
    n = np.random.standard_normal
    idx = np.random.permutation(T)[:J]
    idx2 = np.random.permutation(Z)[:J]
    idx3 = np.stack([np.random.permutation(C)[:J] for _ in range(8)])
    idx4 = np.random.permutation(C)[:O]
    idx5 = np.random.permutation(C)[:O]
    idx6 = np.random.permutation(S)[:N]
    idx7 = np.random.permutation(E)[:O]
    fk = mx_kscale(K)
    ff = mx_kscale(F)
    fr = mx_kscale(R)
    xtp = pack_weight(n((K, T)) / fk[:, None], "e2m1")
    xop = pack_weight(n((F, Z)) / ff[:, None], "e5m2")
    wp = pack_weight(n((K, R)) * 1 / np.sqrt(K) * fk[:, None] * fr, "e5m2")
    w0p = pack_weight(n((F, R)) * 1 / np.sqrt(F) * ff[:, None] * fr, "e4m3")
    vsp = pack_weight(n((R, S)) * 1 / np.sqrt(R) / fr[:, None], "e4m3")
    return {
        "xt_words": xtp[0],
        "xt_scales": xtp[1],
        "xo_words": xop[0],
        "xo_scales": xop[1],
        "w_words": wp[0],
        "w_scales": wp[1],
        "w0_words": w0p[0],
        "w0_scales": w0p[1],
        "sa": (np.random.uniform(0.5, 1.6, (R, 1))).astype(np.float32),
        "sb": (np.random.uniform(0.5, 1.6, (R, 1))).astype(np.float32),
        "vs_words": vsp[0],
        "vs_scales": vsp[1],
        "offs": striped(idx),
        "offs2": striped(idx2),
        "offs3": striped8(idx3),
        "offs4": striped(idx4),
        "offs5": striped(idx5),
        "offs6": striped(idx6),
        "offs7": striped(idx7),
    }


def reference(xt_words, xt_scales, xo_words, xo_scales, w_words, w_scales, w0_words, w0_scales, sa, sb, vs_words, vs_scales, offs, offs2, offs3, offs4, offs5, offs6, offs7):
    idx = unstriped(offs)
    idx2 = unstriped(offs2)
    idx3 = unstriped8(offs3)
    idx4 = unstriped(offs4)
    idx5 = unstriped(offs5)
    idx6 = unstriped(offs6)
    idx7 = unstriped(offs7)
    xtu = unpack_weight(xt_words, xt_scales, "e2m1")
    xou = unpack_weight(xo_words, xo_scales, "e5m2")
    wu = unpack_weight(w_words, w_scales, "e5m2")
    w0u = unpack_weight(w0_words, w0_scales, "e4m3")
    vsu = unpack_weight(vs_words, vs_scales, "e4m3")
    xtidxg = xtu[:, idx]
    xoidx2g = xou[:, idx2]
    a = wu.T @ xtidxg + w0u.T @ xoidx2g
    pw = np.zeros((R, C))
    pw[np.arange(R)[:, None], idx3[np.arange(R) % 512 // 64]] = a
    hid = np.abs(pw[:, idx4] * f64(sa) - pw[:, idx5] * f64(sb))
    vsidx6g = vsu[:, idx6]
    hidq = mxq(hid, 0, "e5m2")
    p = vsidx6g.T @ hidq
    y = np.zeros((N, E))
    y[:, idx7] = p
    return y

@@ -1,0 +1,191 @@
+from contextlib import ExitStack
+
+import concourse.mybir as mybir
+
+K, T, J, R, F, Z, C, O, N, S, E = 512, 1024, 256, 512, 512, 1024, 512, 128, 256, 1024, 1024
+FLOPS = 2 * K * R * J + 2 * F * R * J + 2 * R * N * O
+
+F32 = mybir.dt.float32
+BF16 = mybir.dt.bfloat16
+I32 = mybir.dt.int32
+U32 = mybir.dt.uint32
+U16 = mybir.dt.uint16
+U8 = mybir.dt.uint8
+E4M3 = mybir.dt.float8_e4m3fn_x4
+E5M2 = mybir.dt.float8_e5m2_x4
+E2M1 = mybir.dt.float4_e2m1fn_x4
+COPY = mybir.ActivationFunctionType.Copy
+ALU = mybir.AluOpType
+
+P = 128
+PACK = 4
+HALF = J // 2
+LOW, HIGH = 0, 64
+
+
+def tile_list_ownboard_bank_store_scattered_kernel(
+    tc, xt_words, xt_scales, xo_words, xo_scales, w_words, w_scales, w0_words, w0_scales,
+    sa, sb, vs_words, vs_scales, offs, offs2, offs3, offs4, offs5, offs6, offs7, out,
+):
+    nc = tc.nc
+    with ExitStack() as ctx:
+        pool = ctx.enter_context(tc.tile_pool(name="sbuf", bufs=1))
+        psum = ctx.enter_context(tc.psum_pool(name="psum", bufs=1))
+
+        def load_list(name, src):
+            lst = pool.tile(list(src.shape), U16, name=name)
+            nc.sync.dma_start(lst[:], src)
+            return lst
+
+        def load_words(name, src, dtype, cols, tag=""):
+            words = pool.tile([P, cols], dtype, name=name, tag=tag, align_bytes=64)
+            nc.sync.dma_start(words[:].bitcast(I32), src.bitcast(I32))
+            return words
+
+        def stage_scales(name, src, base, queue):
+            cols = src.shape[2] // 4
+            stage = pool.tile([P, 2, cols], I32, name=name, tag=name, align_bytes=64)
+            nc.vector.memset(stage[base : base + 64], 0)
+            rows = src[0].bitcast(I32).rearrange("(h q r) c -> q r h c", h=2, q=2)
+            for q in range(2):
+                queue.dma_start(stage[base + 32 * q : base + 32 * q + 4], rows[q])
+            return stage
+
+        def spread_scales(name, stage, base):
+            cols = stage.shape[2]
+            plane = pool.tile([P, 4 * cols], U8, name=name, align_bytes=64)
+            for h in ((0, 1) if base == LOW else (1, 0)):
+                nc.vector.tensor_copy(plane[64 * h : 64 * h + 64, :].bitcast(I32), stage[base : base + 64, h, :])
+            return plane
+
+        def spread_in_place(stage, base):
+            stay = base // 64
+            move = 1 - stay
+            nc.vector.tensor_copy(stage[64 * move : 64 * move + 64, stay, :], stage[base : base + 64, move, :])
+            return stage[:, stay, :].bitcast(U8)
+
+        def gather(name, window, offsets, dtype, tag=""):
+            picked = pool.tile([P, 16 * offsets.shape[1]], dtype, name=name, tag=tag, align_bytes=64)
+            nc.vector.tensor_copy(picked[:], window[:].indirect(offsets))
+            return picked
+
+        def deal(name, src, dtype):
+            dealt = pool.tile([P, PACK, P], dtype, name=name, align_bytes=64)
+            nc.vector.tensor_copy(dealt[:], src.rearrange("p (m t) -> p t m", t=PACK))
+            return dealt
+
+        idx = load_list("idx", offs)
+        idx2 = load_list("idx2", offs2)
+        xt_tab = load_words("xt_tab", xt_words[0], U16, T)
+        xt_stage = stage_scales("xt_stage", xt_scales, LOW, nc.sync)
+        xo_stage = stage_scales("xo_stage", xo_scales, HIGH, nc.sync)
+        xo_tab = load_words("xo_tab", xo_words[0].rearrange("p c t -> p (c t)"), U32, Z)
+        w_stage = stage_scales("w_stage", w_scales, LOW, nc.sync)
+        w_tab = load_words("w_tab", w_words[0].rearrange("p c t -> p (c t)"), I32, R, tag="w_tab")
+        w0_stage = stage_scales("w0_stage", w0_scales, HIGH, nc.sync)
+        w0_tab = load_words("w0_tab", w0_words[0].rearrange("p c t -> p (c t)"), I32, R, tag="w0_tab")
+        idx3 = load_list("idx3", offs3)
+        idx4 = load_list("idx4", offs4)
+        idx5 = load_list("idx5", offs5)
+        sa_sb = pool.tile([P, PACK], F32, name="sa_sb")
+        nc.sync.dma_start(sa_sb[:], sa.rearrange("(p t) o -> p (t o)", t=PACK))
+        sb_sb = pool.tile([P, PACK], F32, name="sb_sb")
+        nc.sync.dma_start(sb_sb[:], sb.rearrange("(p t) o -> p (t o)", t=PACK))
+        vs_tab = load_words("vs_tab", vs_words[0].rearrange("p c t -> p (c t)"), U32, S)
+        idx6 = load_list("idx6", offs6)
+        vs_plane = pool.tile([P, S], U8, name="vs_plane", align_bytes=64)
+        nc.vector.memset(vs_plane[:].bitcast(I32), 0)
+        for q in range(4):
+            nc.sync.dma_start(vs_plane[32 * q : 32 * q + 4, :].bitcast(I32), vs_scales[0, 4 * q : 4 * q + 4, :].bitcast(I32))
+        idx7 = load_list("idx7", offs7)
+
+        boards = [pool.tile([P, C], F32, name=f"board{t}") for t in range(PACK)]
+        for board in boards:
+            nc.vector.memset(board[:], 0.0)
+
+        xt_plane = spread_scales("xt_plane", xt_stage, LOW)
+        xo_plane = spread_scales("xo_plane", xo_stage, HIGH)
+
+        def gather_half(h, tags):
+            cols = slice(h * HALF // 16, (h + 1) * HALF // 16)
+            return (
+                gather(f"xt_w{h}", xt_tab, idx[:, cols], U16, tags[0]),
+                gather(f"xt_s{h}", xt_plane, idx[:, cols], U8, tags[1]),
+                gather(f"xo_s{h}", xo_plane, idx2[:, cols], U8, tags[2]),
+                gather(f"xo_w{h}", xo_tab, idx2[:, cols], U32, tags[3]),
+            )
+
+        def scalar_copy(dst, src):
+            nc.scalar.activation(dst, src, COPY)
+
+        def first_stage(name, picked, ts, engine):
+            xt_w, xt_s, xo_s, xo_w = picked
+            acc = psum.tile([P, len(ts), HALF], F32, name=name + "_acc")
+            for i, t in enumerate(ts):
+                nc.tensor.matmul_mx(acc[:, i, :], lhsT=w_w[:, t, :].bitcast(E5M2), lhsT_scale=w_s[:, t, :],
+                                    rhs=xt_w[:].bitcast(E2M1), rhs_scale=xt_s[:], start=True, stop=False)
+                nc.tensor.matmul_mx(acc[:, i, :], lhsT=w0_w[:, t, :].bitcast(E4M3), lhsT_scale=w0_s[:, t, :],
+                                    rhs=xo_w[:].bitcast(E5M2), rhs_scale=xo_s[:], start=False, stop=True)
+            a = pool.tile([P, len(ts), HALF], F32, name=name, tag=name, align_bytes=64)
+            engine(a[:], acc[:])
+            return [a[:, i, :] for i in range(len(ts))]
+
+        def put(t, h, values):
+            cols = slice(h * HALF // 16, (h + 1) * HALF // 16)
+            nc.scalar.activation(boards[t][:].indirect(idx3[:, cols]), values, COPY)
+
+        picked0 = gather_half(0, ("", "", "", ""))
+        w_plane = spread_in_place(w_stage, LOW)
+        w0_plane = spread_in_place(w0_stage, HIGH)
+        w_w = deal("w_w", w_tab[:], I32)
+        w_s = deal("w_s", w_plane, U8)
+        w0_s = deal("w0_s", w0_plane, U8)
+        w0_w = deal("w0_w", w0_tab[:], I32)
+        a_first = first_stage("a01", picked0, [0, 1], scalar_copy)
+        a_first = a_first + first_stage("a23", picked0, [2, 3], nc.vector.tensor_copy)
+        for t in range(PACK):
+            put(t, 0, a_first[t])
+        picked1 = gather_half(1, ("w_tab", "w_stage", "w0_stage", "w0_tab"))
+        a_second = first_stage("a1", picked1, [0, 1, 2, 3], nc.vector.tensor_copy)
+
+        vs_w = gather("vs_w", vs_tab, idx6[:], U32, "w0_tab")
+        vs_s = gather("vs_s", vs_plane, idx6[:], U8, "w0_stage")
+        pages = [pool.tile([P, E], F32, name=f"page{b}", tag=tag, align_bytes=64) for b, tag in enumerate(("a01", "a23"))]
+        for page in pages:
+            nc.vector.memset(page[:], 0.0)
+
+        hid = pool.tile([P, O, PACK], BF16, name="hid", align_bytes=64)
+
+        def look(t):
+            left = pool.tile([P, O], F32, name=f"left{t}")
+            right = pool.tile([P, O], F32, name=f"right{t}")
+            diff = pool.tile([P, O], F32, name=f"diff{t}")
+            nc.scalar.activation(left[:], boards[t][:].indirect(idx4[:]), COPY, scale=sa_sb[:, t : t + 1])
+            nc.scalar.activation(right[:], boards[t][:].indirect(idx5[:]), COPY, scale=sb_sb[:, t : t + 1])
+            nc.vector.tensor_tensor(diff[:], left[:], right[:], ALU.subtract)
+            nc.vector.scalar_tensor_tensor(hid[:, :, t], diff[:], -1.0, diff[:], ALU.mult, ALU.max)
+
+        put(0, 1, a_second[0])
+        for t in range(1, PACK):
+            put(t, 1, a_second[t])
+            look(t - 1)
+        look(PACK - 1)
+
+        hid_w = pool.tile([P, O], U32, name="hid_w", align_bytes=64)
+        hid_s = pool.tile([P, O], U8, name="hid_s", align_bytes=64)
+        nc.vector.quantize_mx(hid_w[:].bitcast(E5M2), hid_s[:], hid[:].rearrange("p o t -> p (o t)"))
+
+        for b in range(N // P):
+            rows = slice(b * P, (b + 1) * P)
+            acc = psum.tile([P, O], F32, name=f"p_acc{b}")
+            nc.tensor.matmul_mx(acc[:], lhsT=vs_w[:, rows].bitcast(E4M3), lhsT_scale=vs_s[:, rows],
+                                rhs=hid_w[:].bitcast(E5M2), rhs_scale=hid_s[:], start=True, stop=True)
+            p = pool.tile([P, O], F32, name=f"p{b}")
+            if b == 0:
+                nc.vector.tensor_copy(p[:], acc[:])
+                nc.vector.tensor_copy(pages[b][:].indirect(idx7[:]), p[:])
+                nc.sync.dma_start(out[rows, :], pages[b][:])
+            else:
+                nc.scalar.copy(p[:], acc[:])
+                nc.scalar.activation(pages[b][:].indirect(idx7[:]), p[:], COPY)
+                nc.scalar.dma_start(out[rows, :], pages[b][:])

@@ -37,9 +37,9 @@ def tile_list_ownboard_bank_store_scattered_kernel(
             nc.sync.dma_start(lst[:], src)
             return lst
 
-        def load_words(name, src, dtype, cols, tag=""):
+        def load_words(name, src, dtype, cols, tag="", queue=nc.sync):
             words = pool.tile([P, cols], dtype, name=name, tag=tag, align_bytes=64)
-            nc.sync.dma_start(words[:].bitcast(I32), src.bitcast(I32))
+            queue.dma_start(words[:].bitcast(I32), src.bitcast(I32))
             return words
 
         def stage_scales(name, src, base, queue):
@@ -69,21 +69,33 @@ def tile_list_ownboard_bank_store_scattered_kernel(
             nc.vector.tensor_copy(picked[:], window[:].indirect(offsets))
             return picked
 
-        def deal(name, src, dtype):
-            dealt = pool.tile([P, PACK, P], dtype, name=name, align_bytes=64)
+        def deal_bytes(name, src):
+            dealt = pool.tile([P, PACK, P], U8, name=name, align_bytes=64)
             nc.vector.tensor_copy(dealt[:], src.rearrange("p (m t) -> p t m", t=PACK))
             return dealt
 
+        def deal_words(name, src):
+            dealt = pool.tile([P, PACK, P], U32, name=name, align_bytes=64)
+            nc.scalar.copy(dealt[:].rearrange("p t m -> p m t"), src.rearrange("p (m t) -> p m t", t=PACK))
+            return dealt
+
+        def load_plane(name, src):
+            plane = pool.tile([P, src.shape[2]], U8, name=name, align_bytes=64)
+            nc.vector.memset(plane[:].bitcast(I32), 0)
+            for q in range(4):
+                nc.sync.dma_start(plane[32 * q : 32 * q + 4, :].bitcast(I32), src[0, 4 * q : 4 * q + 4, :].bitcast(I32))
+            return plane
+
         idx = load_list("idx", offs)
-        idx2 = load_list("idx2", offs2)
         xt_tab = load_words("xt_tab", xt_words[0], U16, T)
-        xt_stage = stage_scales("xt_stage", xt_scales, LOW, nc.sync)
         xo_stage = stage_scales("xo_stage", xo_scales, HIGH, nc.sync)
-        xo_tab = load_words("xo_tab", xo_words[0].rearrange("p c t -> p (c t)"), U32, Z)
         w_stage = stage_scales("w_stage", w_scales, LOW, nc.sync)
-        w_tab = load_words("w_tab", w_words[0].rearrange("p c t -> p (c t)"), I32, R, tag="w_tab")
-        w0_stage = stage_scales("w0_stage", w0_scales, HIGH, nc.sync)
-        w0_tab = load_words("w0_tab", w0_words[0].rearrange("p c t -> p (c t)"), I32, R, tag="w0_tab")
+        w0_stage = stage_scales("w0_stage", w0_scales, LOW, nc.sync)
+        w_tab = load_words("w_tab", w_words[0].rearrange("p c t -> p (c t)"), U32, R)
+        idx2 = load_list("idx2", offs2)
+        w0_tab = load_words("w0_tab", w0_words[0].rearrange("p c t -> p (c t)"), U32, R)
+        xt_plane = load_plane("xt_plane", xt_scales)
+        xo_tab = load_words("xo_tab", xo_words[0].rearrange("p c t -> p (c t)"), U32, Z)
         idx3 = load_list("idx3", offs3)
         idx4 = load_list("idx4", offs4)
         idx5 = load_list("idx5", offs5)
@@ -93,27 +105,21 @@ def tile_list_ownboard_bank_store_scattered_kernel(
         nc.sync.dma_start(sb_sb[:], sb.rearrange("(p t) o -> p (t o)", t=PACK))
         vs_tab = load_words("vs_tab", vs_words[0].rearrange("p c t -> p (c t)"), U32, S)
         idx6 = load_list("idx6", offs6)
-        vs_plane = pool.tile([P, S], U8, name="vs_plane", align_bytes=64)
-        nc.vector.memset(vs_plane[:].bitcast(I32), 0)
-        for q in range(4):
-            nc.sync.dma_start(vs_plane[32 * q : 32 * q + 4, :].bitcast(I32), vs_scales[0, 4 * q : 4 * q + 4, :].bitcast(I32))
+        vs_plane = load_plane("vs_plane", vs_scales)
         idx7 = load_list("idx7", offs7)
 
         boards = [pool.tile([P, C], F32, name=f"board{t}") for t in range(PACK)]
         for board in boards:
             nc.vector.memset(board[:], 0.0)
 
-        xt_plane = spread_scales("xt_plane", xt_stage, LOW)
-        xo_plane = spread_scales("xo_plane", xo_stage, HIGH)
 
-        def gather_half(h, tags):
+        def gather_half(h):
             cols = slice(h * HALF // 16, (h + 1) * HALF // 16)
-            return (
-                gather(f"xt_w{h}", xt_tab, idx[:, cols], U16, tags[0]),
-                gather(f"xt_s{h}", xt_plane, idx[:, cols], U8, tags[1]),
-                gather(f"xo_s{h}", xo_plane, idx2[:, cols], U8, tags[2]),
-                gather(f"xo_w{h}", xo_tab, idx2[:, cols], U32, tags[3]),
-            )
+            xt_w = gather(f"xt_w{h}", xt_tab, idx[:, cols], U16, "xt_w")
+            xo_s = gather(f"xo_s{h}", xo_plane, idx2[:, cols], U8, "xo_s")
+            xt_s = gather(f"xt_s{h}", xt_plane, idx[:, cols], U8, "xt_s")
+            xo_w = gather(f"xo_w{h}", xo_tab, idx2[:, cols], U32, "xo_w")
+            return xt_w, xt_s, xo_s, xo_w
 
         def scalar_copy(dst, src):
             nc.scalar.activation(dst, src, COPY)
@@ -134,23 +140,25 @@ def tile_list_ownboard_bank_store_scattered_kernel(
             cols = slice(h * HALF // 16, (h + 1) * HALF // 16)
             nc.scalar.activation(boards[t][:].indirect(idx3[:, cols]), values, COPY)
 
-        picked0 = gather_half(0, ("", "", "", ""))
+        xo_plane = spread_scales("xo_plane", xo_stage, HIGH)
         w_plane = spread_in_place(w_stage, LOW)
-        w0_plane = spread_in_place(w0_stage, HIGH)
-        w_w = deal("w_w", w_tab[:], I32)
-        w_s = deal("w_s", w_plane, U8)
-        w0_s = deal("w0_s", w0_plane, U8)
-        w0_w = deal("w0_w", w0_tab[:], I32)
-        a_first = first_stage("a01", picked0, [0, 1], scalar_copy)
+        w0_plane = spread_in_place(w0_stage, LOW)
+        w_s = deal_bytes("w_s", w_plane)
+        w0_s = deal_bytes("w0_s", w0_plane)
+        w_w = deal_words("w_w", w_tab[:])
+        w0_w = deal_words("w0_w", w0_tab[:])
+        picked0 = gather_half(0)
+        a_first = first_stage("a0", picked0, [0], scalar_copy)
+        a_first = a_first + first_stage("a1", picked0, [1], nc.vector.tensor_copy)
         a_first = a_first + first_stage("a23", picked0, [2, 3], nc.vector.tensor_copy)
         for t in range(PACK):
             put(t, 0, a_first[t])
-        picked1 = gather_half(1, ("w_tab", "w_stage", "w0_stage", "w0_tab"))
-        a_second = first_stage("a1", picked1, [0, 1, 2, 3], nc.vector.tensor_copy)
+        picked1 = gather_half(1)
+        a_second = first_stage("a_second", picked1, [0, 1, 2, 3], nc.vector.tensor_copy)
 
-        vs_w = gather("vs_w", vs_tab, idx6[:], U32, "w0_tab")
-        vs_s = gather("vs_s", vs_plane, idx6[:], U8, "w0_stage")
-        pages = [pool.tile([P, E], F32, name=f"page{b}", tag=tag, align_bytes=64) for b, tag in enumerate(("a01", "a23"))]
+        vs_w = gather("vs_w", vs_tab, idx6[:], U32, "xo_w")
+        vs_s = gather("vs_s", vs_plane, idx6[:], U8, "xo_s")
+        pages = [pool.tile([P, E], F32, name=f"page{b}", tag=tag, align_bytes=64) for b, tag in enumerate(("a1", "a23"))]
         for page in pages:
             nc.vector.memset(page[:], 0.0)
 

@@ -15,6 +15,7 @@ E4M3 = mybir.dt.float8_e4m3fn_x4
 E5M2 = mybir.dt.float8_e5m2_x4
 E2M1 = mybir.dt.float4_e2m1fn_x4
 COPY = mybir.ActivationFunctionType.Copy
+ABS = mybir.ActivationFunctionType.Abs
 ALU = mybir.AluOpType
 
 P = 128
@@ -103,9 +104,9 @@ def tile_list_ownboard_bank_store_scattered_kernel(
         nc.sync.dma_start(sa_sb[:], sa.rearrange("(p t) o -> p (t o)", t=PACK))
         sb_sb = pool.tile([P, PACK], F32, name="sb_sb")
         nc.sync.dma_start(sb_sb[:], sb.rearrange("(p t) o -> p (t o)", t=PACK))
-        vs_tab = load_words("vs_tab", vs_words[0].rearrange("p c t -> p (c t)"), U32, S)
         idx6 = load_list("idx6", offs6)
         vs_plane = load_plane("vs_plane", vs_scales)
+        vs_tab = load_words("vs_tab", vs_words[0].rearrange("p c t -> p (c t)"), U32, S, tag="vs_tab")
         idx7 = load_list("idx7", offs7)
 
         boards = [pool.tile([P, C], F32, name=f"board{t}") for t in range(PACK)]
@@ -154,30 +155,36 @@ def tile_list_ownboard_bank_store_scattered_kernel(
         for t in range(PACK):
             put(t, 0, a_first[t])
         picked1 = gather_half(1)
-        a_second = first_stage("a_second", picked1, [0, 1, 2, 3], nc.vector.tensor_copy)
+        a_second = first_stage("b01", picked1, [0, 1], nc.vector.tensor_copy)
+        a_second = a_second + first_stage("b23", picked1, [2, 3], nc.vector.tensor_copy)
 
-        vs_w = gather("vs_w", vs_tab, idx6[:], U32, "xo_w")
         vs_s = gather("vs_s", vs_plane, idx6[:], U8, "xo_s")
+        vs_w = gather("vs_w", vs_tab, idx6[:], U32, "xo_w")
         pages = [pool.tile([P, E], F32, name=f"page{b}", tag=tag, align_bytes=64) for b, tag in enumerate(("a1", "a23"))]
         for page in pages:
             nc.vector.memset(page[:], 0.0)
 
         hid = pool.tile([P, O, PACK], BF16, name="hid", align_bytes=64)
 
+        diff = pool.tile([P, PACK, O], F32, name="diff", tag="vs_tab", align_bytes=64)
+
         def look(t):
             left = pool.tile([P, O], F32, name=f"left{t}")
             right = pool.tile([P, O], F32, name=f"right{t}")
-            diff = pool.tile([P, O], F32, name=f"diff{t}")
             nc.scalar.activation(left[:], boards[t][:].indirect(idx4[:]), COPY, scale=sa_sb[:, t : t + 1])
             nc.scalar.activation(right[:], boards[t][:].indirect(idx5[:]), COPY, scale=sb_sb[:, t : t + 1])
-            nc.vector.tensor_tensor(diff[:], left[:], right[:], ALU.subtract)
-            nc.vector.scalar_tensor_tensor(hid[:, :, t], diff[:], -1.0, diff[:], ALU.mult, ALU.max)
+            nc.vector.tensor_tensor(diff[:, t, :], left[:], right[:], ALU.subtract)
 
         put(0, 1, a_second[0])
         for t in range(1, PACK):
             put(t, 1, a_second[t])
             look(t - 1)
         look(PACK - 1)
+
+        woven = diff[:].rearrange("p t o -> p o t")
+        first, second = slice(0, O // 2), slice(O // 2, O)
+        nc.vector.scalar_tensor_tensor(hid[:, first, :], woven[:, first, :], -1.0, woven[:, first, :], ALU.mult, ALU.max)
+        nc.scalar.activation(hid[:, second, :], woven[:, second, :], ABS)
 
         hid_w = pool.tile([P, O], U32, name="hid_w", align_bytes=64)
         hid_s = pool.tile([P, O], U8, name="hid_s", align_bytes=64)

@@ -20,8 +20,11 @@ ALU = mybir.AluOpType
 
 P = 128
 PACK = 4
-HALF = J // 2
-LOW, HIGH = 0, 64
+GROUP = 16
+QUAD = 32
+HALF_P = P // 2
+HALF_J = J // 2
+ALIGN = 64
 
 
 def tile_list_ownboard_bank_store_scattered_kernel(
@@ -34,69 +37,64 @@ def tile_list_ownboard_bank_store_scattered_kernel(
         psum = ctx.enter_context(tc.psum_pool(name="psum", bufs=1))
 
         def load_list(name, src):
-            lst = pool.tile(list(src.shape), U16, name=name)
-            nc.sync.dma_start(lst[:], src)
-            return lst
+            entries = pool.tile(list(src.shape), U16, name=name)
+            nc.sync.dma_start(entries[:], src)
+            return entries
 
-        def load_words(name, src, dtype, cols, tag="", queue=nc.sync):
-            words = pool.tile([P, cols], dtype, name=name, tag=tag, align_bytes=64)
-            queue.dma_start(words[:].bitcast(I32), src.bitcast(I32))
+        def load_words(name, src, dtype, cols):
+            words = pool.tile([P, cols], dtype, name=name, tag=name, align_bytes=ALIGN)
+            nc.sync.dma_start(words[:].bitcast(I32), src.bitcast(I32))
             return words
 
-        def stage_scales(name, src, base, queue):
-            cols = src.shape[2] // 4
-            stage = pool.tile([P, 2, cols], I32, name=name, tag=name, align_bytes=64)
-            nc.vector.memset(stage[base : base + 64], 0)
-            rows = src[0].bitcast(I32).rearrange("(h q r) c -> q r h c", h=2, q=2)
-            for q in range(2):
-                queue.dma_start(stage[base + 32 * q : base + 32 * q + 4], rows[q])
-            return stage
+        def fp8_words(src):
+            return src[0].rearrange("p c t -> p (c t)")
 
-        def spread_scales(name, stage, base):
-            cols = stage.shape[2]
-            plane = pool.tile([P, 4 * cols], U8, name=name, align_bytes=64)
-            for h in ((0, 1) if base == LOW else (1, 0)):
-                nc.vector.tensor_copy(plane[64 * h : 64 * h + 64, :].bitcast(I32), stage[base : base + 64, h, :])
+        def load_plane(name, src):
+            plane = pool.tile([P, src.shape[2]], U8, name=name, align_bytes=ALIGN)
+            nc.vector.memset(plane[:].bitcast(I32), 0)
+            for q in range(P // QUAD):
+                nc.sync.dma_start(
+                    plane[QUAD * q : QUAD * q + 4, :].bitcast(I32), src[0, 4 * q : 4 * q + 4, :].bitcast(I32)
+                )
             return plane
 
-        def spread_in_place(stage, base):
-            stay = base // 64
-            move = 1 - stay
-            nc.vector.tensor_copy(stage[64 * move : 64 * move + 64, stay, :], stage[base : base + 64, move, :])
-            return stage[:, stay, :].bitcast(U8)
+        def stage_scales(name, src, base, clearer):
+            stage = pool.tile([P, 2, src.shape[2] // 4], I32, name=name, align_bytes=ALIGN)
+            clearer.memset(stage[base : base + HALF_P], 0)
+            rows = src[0].bitcast(I32).rearrange("(h q r) c -> q r h c", h=2, q=2)
+            for q in range(2):
+                nc.sync.dma_start(stage[base + QUAD * q : base + QUAD * q + 4], rows[q])
+            return stage
 
-        def gather(name, window, offsets, dtype, tag=""):
-            picked = pool.tile([P, 16 * offsets.shape[1]], dtype, name=name, tag=tag, align_bytes=64)
+        def finish_plane_in_place(stage):
+            nc.vector.tensor_copy(stage[HALF_P:P, 0, :], stage[0:HALF_P, 1, :])
+            return stage[:, 0, :].bitcast(U8)
+
+        def gather(name, window, offsets, dtype, tag):
+            picked = pool.tile([P, GROUP * offsets.shape[1]], dtype, name=name, tag=tag, align_bytes=ALIGN)
             nc.vector.tensor_copy(picked[:], window[:].indirect(offsets))
             return picked
 
         def deal_bytes(name, src):
-            dealt = pool.tile([P, PACK, P], U8, name=name, align_bytes=64)
+            dealt = pool.tile([P, PACK, P], U8, name=name, align_bytes=ALIGN)
             nc.vector.tensor_copy(dealt[:], src.rearrange("p (m t) -> p t m", t=PACK))
             return dealt
 
         def deal_words(name, src):
-            dealt = pool.tile([P, PACK, P], U32, name=name, align_bytes=64)
+            dealt = pool.tile([P, PACK, P], U32, name=name, align_bytes=ALIGN)
             nc.scalar.copy(dealt[:].rearrange("p t m -> p m t"), src.rearrange("p (m t) -> p m t", t=PACK))
             return dealt
 
-        def load_plane(name, src):
-            plane = pool.tile([P, src.shape[2]], U8, name=name, align_bytes=64)
-            nc.vector.memset(plane[:].bitcast(I32), 0)
-            for q in range(4):
-                nc.sync.dma_start(plane[32 * q : 32 * q + 4, :].bitcast(I32), src[0, 4 * q : 4 * q + 4, :].bitcast(I32))
-            return plane
-
         idx = load_list("idx", offs)
         xt_tab = load_words("xt_tab", xt_words[0], U16, T)
-        xo_stage = stage_scales("xo_stage", xo_scales, HIGH, nc.sync)
-        w_stage = stage_scales("w_stage", w_scales, LOW, nc.sync)
-        w0_stage = stage_scales("w0_stage", w0_scales, LOW, nc.sync)
-        w_tab = load_words("w_tab", w_words[0].rearrange("p c t -> p (c t)"), U32, R)
+        w_stage = stage_scales("w_stage", w_scales, 0, nc.vector)
+        w0_stage = stage_scales("w0_stage", w0_scales, 0, nc.vector)
+        xo_stage = stage_scales("xo_stage", xo_scales, HALF_P, nc.gpsimd)
+        w_tab = load_words("w_tab", fp8_words(w_words), U32, R)
         idx2 = load_list("idx2", offs2)
-        w0_tab = load_words("w0_tab", w0_words[0].rearrange("p c t -> p (c t)"), U32, R)
+        w0_tab = load_words("w0_tab", fp8_words(w0_words), U32, R)
         xt_plane = load_plane("xt_plane", xt_scales)
-        xo_tab = load_words("xo_tab", xo_words[0].rearrange("p c t -> p (c t)"), U32, Z)
+        xo_tab = load_words("xo_tab", fp8_words(xo_words), U32, Z)
         idx3 = load_list("idx3", offs3)
         idx4 = load_list("idx4", offs4)
         idx5 = load_list("idx5", offs5)
@@ -106,67 +104,70 @@ def tile_list_ownboard_bank_store_scattered_kernel(
         nc.sync.dma_start(sb_sb[:], sb.rearrange("(p t) o -> p (t o)", t=PACK))
         idx6 = load_list("idx6", offs6)
         vs_plane = load_plane("vs_plane", vs_scales)
-        vs_tab = load_words("vs_tab", vs_words[0].rearrange("p c t -> p (c t)"), U32, S, tag="vs_tab")
+        vs_tab = load_words("vs_tab", fp8_words(vs_words), U32, S)
         idx7 = load_list("idx7", offs7)
 
         boards = [pool.tile([P, C], F32, name=f"board{t}") for t in range(PACK)]
         for board in boards:
             nc.vector.memset(board[:], 0.0)
 
-
-        def gather_half(h):
-            cols = slice(h * HALF // 16, (h + 1) * HALF // 16)
-            xt_w = gather(f"xt_w{h}", xt_tab, idx[:, cols], U16, "xt_w")
-            xo_s = gather(f"xo_s{h}", xo_plane, idx2[:, cols], U8, "xo_s")
-            xt_s = gather(f"xt_s{h}", xt_plane, idx[:, cols], U8, "xt_s")
-            xo_w = gather(f"xo_w{h}", xo_tab, idx2[:, cols], U32, "xo_w")
-            return xt_w, xt_s, xo_s, xo_w
-
-        def scalar_copy(dst, src):
-            nc.scalar.activation(dst, src, COPY)
-
-        def first_stage(name, picked, ts, engine):
-            xt_w, xt_s, xo_s, xo_w = picked
-            acc = psum.tile([P, len(ts), HALF], F32, name=name + "_acc")
-            for i, t in enumerate(ts):
-                nc.tensor.matmul_mx(acc[:, i, :], lhsT=w_w[:, t, :].bitcast(E5M2), lhsT_scale=w_s[:, t, :],
-                                    rhs=xt_w[:].bitcast(E2M1), rhs_scale=xt_s[:], start=True, stop=False)
-                nc.tensor.matmul_mx(acc[:, i, :], lhsT=w0_w[:, t, :].bitcast(E4M3), lhsT_scale=w0_s[:, t, :],
-                                    rhs=xo_w[:].bitcast(E5M2), rhs_scale=xo_s[:], start=False, stop=True)
-            a = pool.tile([P, len(ts), HALF], F32, name=name, tag=name, align_bytes=64)
-            engine(a[:], acc[:])
-            return [a[:, i, :] for i in range(len(ts))]
-
-        def put(t, h, values):
-            cols = slice(h * HALF // 16, (h + 1) * HALF // 16)
-            nc.scalar.activation(boards[t][:].indirect(idx3[:, cols]), values, COPY)
-
-        xo_plane = spread_scales("xo_plane", xo_stage, HIGH)
-        w_plane = spread_in_place(w_stage, LOW)
-        w0_plane = spread_in_place(w0_stage, LOW)
+        w_plane = finish_plane_in_place(w_stage)
+        w0_plane = finish_plane_in_place(w0_stage)
+        xo_plane = pool.tile([P, Z], U8, name="xo_plane", align_bytes=ALIGN)
+        nc.vector.tensor_copy(xo_plane[HALF_P:P, :].bitcast(I32), xo_stage[HALF_P:P, 1, :])
+        nc.vector.tensor_copy(xo_plane[0:HALF_P, :].bitcast(I32), xo_stage[HALF_P:P, 0, :])
         w_s = deal_bytes("w_s", w_plane)
         w0_s = deal_bytes("w0_s", w0_plane)
         w_w = deal_words("w_w", w_tab[:])
         w0_w = deal_words("w0_w", w0_tab[:])
-        picked0 = gather_half(0)
-        a_first = first_stage("a0", picked0, [0], scalar_copy)
-        a_first = a_first + first_stage("a1", picked0, [1], nc.vector.tensor_copy)
-        a_first = a_first + first_stage("a23", picked0, [2, 3], nc.vector.tensor_copy)
+
+        def slots(half):
+            return slice(half * HALF_J // GROUP, (half + 1) * HALF_J // GROUP)
+
+        def scalar_copy(dst, src):
+            nc.scalar.activation(dst, src, COPY)
+
+        def first_stage(half, first_copy):
+            xt_w = gather(f"xt_w{half}", xt_tab, idx[:, slots(half)], U16, "xt_w")
+            xt_s = gather(f"xt_s{half}", xt_plane, idx[:, slots(half)], U8, "xt_s")
+            xo_s = gather(f"xo_s{half}", xo_plane, idx2[:, slots(half)], U8, "xo_s")
+            xo_w = gather(f"xo_w{half}", xo_tab, idx2[:, slots(half)], U32, "xo_w")
+            parts = []
+            for bank, copy in (((0,), first_copy), ((1,), nc.vector.tensor_copy), ((2, 3), nc.vector.tensor_copy)):
+                name = f"a{half}_{bank[0]}"
+                acc = psum.tile([P, len(bank), HALF_J], F32, name=name + "_acc")
+                for i, t in enumerate(bank):
+                    nc.tensor.matmul_mx(
+                        acc[:, i, :], lhsT=w_w[:, t, :].bitcast(E5M2), lhsT_scale=w_s[:, t, :],
+                        rhs=xt_w[:].bitcast(E2M1), rhs_scale=xt_s[:], start=True, stop=False,
+                    )
+                    nc.tensor.matmul_mx(
+                        acc[:, i, :], lhsT=w0_w[:, t, :].bitcast(E4M3), lhsT_scale=w0_s[:, t, :],
+                        rhs=xo_w[:].bitcast(E5M2), rhs_scale=xo_s[:], start=False, stop=True,
+                    )
+                a = pool.tile([P, len(bank), HALF_J], F32, name=name, tag=name, align_bytes=ALIGN)
+                copy(a[:], acc[:])
+                parts.extend([a[:, i, :] for i in range(len(bank))])
+            return parts
+
+        def put(t, half, values):
+            nc.scalar.activation(boards[t][:].indirect(idx3[:, slots(half)]), values, COPY)
+
+        a_first = first_stage(0, scalar_copy)
         for t in range(PACK):
             put(t, 0, a_first[t])
-        picked1 = gather_half(1)
-        a_second = first_stage("b01", picked1, [0, 1], nc.vector.tensor_copy)
-        a_second = a_second + first_stage("b23", picked1, [2, 3], nc.vector.tensor_copy)
+        a_second = first_stage(1, nc.vector.tensor_copy)
 
         vs_s = gather("vs_s", vs_plane, idx6[:], U8, "xo_s")
         vs_w = gather("vs_w", vs_tab, idx6[:], U32, "xo_w")
-        pages = [pool.tile([P, E], F32, name=f"page{b}", tag=tag, align_bytes=64) for b, tag in enumerate(("a1", "a23"))]
+        pages = [
+            pool.tile([P, E], F32, name=f"page{b}", tag=tag, align_bytes=ALIGN) for b, tag in enumerate(("a0_1", "a0_2"))
+        ]
         for page in pages:
             nc.vector.memset(page[:], 0.0)
 
-        hid = pool.tile([P, O, PACK], BF16, name="hid", align_bytes=64)
-
-        diff = pool.tile([P, PACK, O], F32, name="diff", tag="vs_tab", align_bytes=64)
+        hid = pool.tile([P, O, PACK], BF16, name="hid", align_bytes=ALIGN)
+        diff = pool.tile([P, PACK, O], F32, name="diff", tag="vs_tab", align_bytes=ALIGN)
 
         def look(t):
             left = pool.tile([P, O], F32, name=f"left{t}")
@@ -182,25 +183,26 @@ def tile_list_ownboard_bank_store_scattered_kernel(
         look(PACK - 1)
 
         woven = diff[:].rearrange("p t o -> p o t")
-        first, second = slice(0, O // 2), slice(O // 2, O)
-        nc.vector.scalar_tensor_tensor(hid[:, first, :], woven[:, first, :], -1.0, woven[:, first, :], ALU.mult, ALU.max)
-        nc.scalar.activation(hid[:, second, :], woven[:, second, :], ABS)
+        lower, upper = slice(0, O // 2), slice(O // 2, O)
+        nc.vector.scalar_tensor_tensor(hid[:, lower, :], woven[:, lower, :], -1.0, woven[:, lower, :], ALU.mult, ALU.max)
+        nc.scalar.activation(hid[:, upper, :], woven[:, upper, :], ABS)
 
-        hid_w = pool.tile([P, O], U32, name="hid_w", align_bytes=64)
-        hid_s = pool.tile([P, O], U8, name="hid_s", align_bytes=64)
+        hid_w = pool.tile([P, O], U32, name="hid_w", align_bytes=ALIGN)
+        hid_s = pool.tile([P, O], U8, name="hid_s", align_bytes=ALIGN)
         nc.vector.quantize_mx(hid_w[:].bitcast(E5M2), hid_s[:], hid[:].rearrange("p o t -> p (o t)"))
 
-        for b in range(N // P):
+        finishers = (
+            (nc.vector.tensor_copy, nc.vector.tensor_copy, nc.sync),
+            (nc.scalar.copy, scalar_copy, nc.scalar),
+        )
+        for b, (copy, scatter, queue) in enumerate(finishers):
             rows = slice(b * P, (b + 1) * P)
             acc = psum.tile([P, O], F32, name=f"p_acc{b}")
-            nc.tensor.matmul_mx(acc[:], lhsT=vs_w[:, rows].bitcast(E4M3), lhsT_scale=vs_s[:, rows],
-                                rhs=hid_w[:].bitcast(E5M2), rhs_scale=hid_s[:], start=True, stop=True)
+            nc.tensor.matmul_mx(
+                acc[:], lhsT=vs_w[:, rows].bitcast(E4M3), lhsT_scale=vs_s[:, rows],
+                rhs=hid_w[:].bitcast(E5M2), rhs_scale=hid_s[:], start=True, stop=True,
+            )
             p = pool.tile([P, O], F32, name=f"p{b}")
-            if b == 0:
-                nc.vector.tensor_copy(p[:], acc[:])
-                nc.vector.tensor_copy(pages[b][:].indirect(idx7[:]), p[:])
-                nc.sync.dma_start(out[rows, :], pages[b][:])
-            else:
-                nc.scalar.copy(p[:], acc[:])
-                nc.scalar.activation(pages[b][:].indirect(idx7[:]), p[:], COPY)
-                nc.scalar.dma_start(out[rows, :], pages[b][:])
+            copy(p[:], acc[:])
+            scatter(pages[b][:].indirect(idx7[:]), p[:])
+            queue.dma_start(out[rows, :], pages[b][:])

from contextlib import ExitStack

import concourse.mybir as mybir

K, T, J, R, F, Z, C, O, N, S, E = 512, 1024, 256, 512, 512, 1024, 512, 128, 256, 1024, 1024
FLOPS = 2 * K * R * J + 2 * F * R * J + 2 * R * N * O

F32 = mybir.dt.float32
BF16 = mybir.dt.bfloat16
I32 = mybir.dt.int32
U32 = mybir.dt.uint32
U16 = mybir.dt.uint16
U8 = mybir.dt.uint8
E4M3 = mybir.dt.float8_e4m3fn_x4
E5M2 = mybir.dt.float8_e5m2_x4
E2M1 = mybir.dt.float4_e2m1fn_x4
COPY = mybir.ActivationFunctionType.Copy
ABS = mybir.ActivationFunctionType.Abs
ALU = mybir.AluOpType

P = 128
PACK = 4
GROUP = 16
QUAD = 32
HALF_P = P // 2
HALF_J = J // 2
ALIGN = 64


def tile_list_ownboard_bank_store_scattered_kernel(
    tc, xt_words, xt_scales, xo_words, xo_scales, w_words, w_scales, w0_words, w0_scales,
    sa, sb, vs_words, vs_scales, offs, offs2, offs3, offs4, offs5, offs6, offs7, out,
):
    nc = tc.nc
    with ExitStack() as ctx:
        pool = ctx.enter_context(tc.tile_pool(name="sbuf", bufs=1))
        psum = ctx.enter_context(tc.psum_pool(name="psum", bufs=1))

        def load_list(name, src):
            entries = pool.tile(list(src.shape), U16, name=name)
            nc.sync.dma_start(entries[:], src)
            return entries

        def load_words(name, src, dtype, cols):
            words = pool.tile([P, cols], dtype, name=name, tag=name, align_bytes=ALIGN)
            nc.sync.dma_start(words[:].bitcast(I32), src.bitcast(I32))
            return words

        def fp8_words(src):
            return src[0].rearrange("p c t -> p (c t)")

        def load_plane(name, src):
            plane = pool.tile([P, src.shape[2]], U8, name=name, align_bytes=ALIGN)
            nc.vector.memset(plane[:].bitcast(I32), 0)
            for q in range(P // QUAD):
                nc.sync.dma_start(
                    plane[QUAD * q : QUAD * q + 4, :].bitcast(I32), src[0, 4 * q : 4 * q + 4, :].bitcast(I32)
                )
            return plane

        def stage_scales(name, src, base, clearer):
            stage = pool.tile([P, 2, src.shape[2] // 4], I32, name=name, align_bytes=ALIGN)
            clearer.memset(stage[base : base + HALF_P], 0)
            rows = src[0].bitcast(I32).rearrange("(h q r) c -> q r h c", h=2, q=2)
            for q in range(2):
                nc.sync.dma_start(stage[base + QUAD * q : base + QUAD * q + 4], rows[q])
            return stage

        def finish_plane_in_place(stage):
            nc.vector.tensor_copy(stage[HALF_P:P, 0, :], stage[0:HALF_P, 1, :])
            return stage[:, 0, :].bitcast(U8)

        def gather(name, window, offsets, dtype, tag):
            picked = pool.tile([P, GROUP * offsets.shape[1]], dtype, name=name, tag=tag, align_bytes=ALIGN)
            nc.vector.tensor_copy(picked[:], window[:].indirect(offsets))
            return picked

        def deal_bytes(name, src):
            dealt = pool.tile([P, PACK, P], U8, name=name, align_bytes=ALIGN)
            nc.vector.tensor_copy(dealt[:], src.rearrange("p (m t) -> p t m", t=PACK))
            return dealt

        def deal_words(name, src):
            dealt = pool.tile([P, PACK, P], U32, name=name, align_bytes=ALIGN)
            nc.scalar.copy(dealt[:].rearrange("p t m -> p m t"), src.rearrange("p (m t) -> p m t", t=PACK))
            return dealt

        idx = load_list("idx", offs)
        xt_tab = load_words("xt_tab", xt_words[0], U16, T)
        w_stage = stage_scales("w_stage", w_scales, 0, nc.vector)
        w0_stage = stage_scales("w0_stage", w0_scales, 0, nc.vector)
        xo_stage = stage_scales("xo_stage", xo_scales, HALF_P, nc.gpsimd)
        w_tab = load_words("w_tab", fp8_words(w_words), U32, R)
        idx2 = load_list("idx2", offs2)
        w0_tab = load_words("w0_tab", fp8_words(w0_words), U32, R)
        xt_plane = load_plane("xt_plane", xt_scales)
        xo_tab = load_words("xo_tab", fp8_words(xo_words), U32, Z)
        idx3 = load_list("idx3", offs3)
        idx4 = load_list("idx4", offs4)
        idx5 = load_list("idx5", offs5)
        sa_sb = pool.tile([P, PACK], F32, name="sa_sb")
        nc.sync.dma_start(sa_sb[:], sa.rearrange("(p t) o -> p (t o)", t=PACK))
        sb_sb = pool.tile([P, PACK], F32, name="sb_sb")
        nc.sync.dma_start(sb_sb[:], sb.rearrange("(p t) o -> p (t o)", t=PACK))
        idx6 = load_list("idx6", offs6)
        vs_plane = load_plane("vs_plane", vs_scales)
        vs_tab = load_words("vs_tab", fp8_words(vs_words), U32, S)
        idx7 = load_list("idx7", offs7)

        boards = [pool.tile([P, C], F32, name=f"board{t}") for t in range(PACK)]
        for board in boards:
            nc.vector.memset(board[:], 0.0)

        w_plane = finish_plane_in_place(w_stage)
        w0_plane = finish_plane_in_place(w0_stage)
        xo_plane = pool.tile([P, Z], U8, name="xo_plane", align_bytes=ALIGN)
        nc.vector.tensor_copy(xo_plane[HALF_P:P, :].bitcast(I32), xo_stage[HALF_P:P, 1, :])
        nc.vector.tensor_copy(xo_plane[0:HALF_P, :].bitcast(I32), xo_stage[HALF_P:P, 0, :])
        w_s = deal_bytes("w_s", w_plane)
        w0_s = deal_bytes("w0_s", w0_plane)
        w_w = deal_words("w_w", w_tab[:])
        w0_w = deal_words("w0_w", w0_tab[:])

        def slots(half):
            return slice(half * HALF_J // GROUP, (half + 1) * HALF_J // GROUP)

        def scalar_copy(dst, src):
            nc.scalar.activation(dst, src, COPY)

        def first_stage(half, first_copy):
            xt_w = gather(f"xt_w{half}", xt_tab, idx[:, slots(half)], U16, "xt_w")
            xt_s = gather(f"xt_s{half}", xt_plane, idx[:, slots(half)], U8, "xt_s")
            xo_s = gather(f"xo_s{half}", xo_plane, idx2[:, slots(half)], U8, "xo_s")
            xo_w = gather(f"xo_w{half}", xo_tab, idx2[:, slots(half)], U32, "xo_w")
            parts = []
            for bank, copy in (((0,), first_copy), ((1,), nc.vector.tensor_copy), ((2, 3), nc.vector.tensor_copy)):
                name = f"a{half}_{bank[0]}"
                acc = psum.tile([P, len(bank), HALF_J], F32, name=name + "_acc")
                for i, t in enumerate(bank):
                    nc.tensor.matmul_mx(
                        acc[:, i, :], lhsT=w_w[:, t, :].bitcast(E5M2), lhsT_scale=w_s[:, t, :],
                        rhs=xt_w[:].bitcast(E2M1), rhs_scale=xt_s[:], start=True, stop=False,
                    )
                    nc.tensor.matmul_mx(
                        acc[:, i, :], lhsT=w0_w[:, t, :].bitcast(E4M3), lhsT_scale=w0_s[:, t, :],
                        rhs=xo_w[:].bitcast(E5M2), rhs_scale=xo_s[:], start=False, stop=True,
                    )
                a = pool.tile([P, len(bank), HALF_J], F32, name=name, tag=name, align_bytes=ALIGN)
                copy(a[:], acc[:])
                parts.extend([a[:, i, :] for i in range(len(bank))])
            return parts

        def put(t, half, values):
            nc.scalar.activation(boards[t][:].indirect(idx3[:, slots(half)]), values, COPY)

        a_first = first_stage(0, scalar_copy)
        for t in range(PACK):
            put(t, 0, a_first[t])
        a_second = first_stage(1, nc.vector.tensor_copy)

        vs_s = gather("vs_s", vs_plane, idx6[:], U8, "xo_s")
        vs_w = gather("vs_w", vs_tab, idx6[:], U32, "xo_w")
        pages = [
            pool.tile([P, E], F32, name=f"page{b}", tag=tag, align_bytes=ALIGN) for b, tag in enumerate(("a0_1", "a0_2"))
        ]
        for page in pages:
            nc.vector.memset(page[:], 0.0)

        hid = pool.tile([P, O, PACK], BF16, name="hid", align_bytes=ALIGN)
        diff = pool.tile([P, PACK, O], F32, name="diff", tag="vs_tab", align_bytes=ALIGN)

        def look(t):
            left = pool.tile([P, O], F32, name=f"left{t}")
            right = pool.tile([P, O], F32, name=f"right{t}")
            nc.scalar.activation(left[:], boards[t][:].indirect(idx4[:]), COPY, scale=sa_sb[:, t : t + 1])
            nc.scalar.activation(right[:], boards[t][:].indirect(idx5[:]), COPY, scale=sb_sb[:, t : t + 1])
            nc.vector.tensor_tensor(diff[:, t, :], left[:], right[:], ALU.subtract)

        put(0, 1, a_second[0])
        for t in range(1, PACK):
            put(t, 1, a_second[t])
            look(t - 1)
        look(PACK - 1)

        woven = diff[:].rearrange("p t o -> p o t")
        lower, upper = slice(0, O // 2), slice(O // 2, O)
        nc.vector.scalar_tensor_tensor(hid[:, lower, :], woven[:, lower, :], -1.0, woven[:, lower, :], ALU.mult, ALU.max)
        nc.scalar.activation(hid[:, upper, :], woven[:, upper, :], ABS)

        hid_w = pool.tile([P, O], U32, name="hid_w", align_bytes=ALIGN)
        hid_s = pool.tile([P, O], U8, name="hid_s", align_bytes=ALIGN)
        nc.vector.quantize_mx(hid_w[:].bitcast(E5M2), hid_s[:], hid[:].rearrange("p o t -> p (o t)"))

        finishers = (
            (nc.vector.tensor_copy, nc.vector.tensor_copy, nc.sync),
            (nc.scalar.copy, scalar_copy, nc.scalar),
        )
        for b, (copy, scatter, queue) in enumerate(finishers):
            rows = slice(b * P, (b + 1) * P)
            acc = psum.tile([P, O], F32, name=f"p_acc{b}")
            nc.tensor.matmul_mx(
                acc[:], lhsT=vs_w[:, rows].bitcast(E4M3), lhsT_scale=vs_s[:, rows],
                rhs=hid_w[:].bitcast(E5M2), rhs_scale=hid_s[:], start=True, stop=True,
            )
            p = pool.tile([P, O], F32, name=f"p{b}")
            copy(p[:], acc[:])
            scatter(pages[b][:].indirect(idx7[:]), p[:])
            queue.dma_start(out[rows, :], pages[b][:])
